import numpy as np, ml_dtypes
CORES = [18,19,22,23,26,27,30,31,98,99,102,103,106,107,110,111]
N = 16
def setup_inputs(rng):
    return {"x": rng.standard_normal((N, 128, 512), dtype=np.float32).astype(ml_dtypes.bfloat16)}
def reference(x):
    g = np.concatenate(list(x), axis=1)
    return {"y": np.broadcast_to(g, (N,) + g.shape)}

@@ -1,0 +1,72 @@
+from concourse.bass import DstId, RemoteDMATransfer
+
+W = 512
+RK = (2, 3, 6, 7)
+HK = (0, 1, 4, 5)
+
+SCRATCH = {
+    "land": ("sbuf", [128, 16 * W], "bfloat16"),
+    "xd": ("dram", [128, W], "bfloat16"),
+    "hbuf": ("dram", [4, 128, W], "bfloat16"),
+}
+SEMAPHORES = ["ldx", "ldl", "sent", "st_a", "st_b",
+              "h0", "h1", "h2", "h3",
+              "g0", "g1", "g2", "g3"]
+
+
+def rank_program(g, core, T, topo):
+    chips = sorted(set(topo.chip(c) for c in T.cores))
+    ch, k = topo.chip(core), core % 8
+    if ch not in chips:
+        return
+    mate = ch ^ 1
+    plane = [c for c in chips if topo.same_plane(c, ch)][0]
+    diag = plane ^ 1
+    n_of = dict((c, n) for n, c in enumerate(chips))
+    hsem = lambda c: T.sem["h%d" % n_of[c]]
+    gsem = lambda c: T.sem["g%d" % n_of[c]]
+
+    def did(c):
+        rid, pid, _se = topo.addr(c)
+        return DstId(rid=rid, pnc=pid)
+
+    rank = T.rank_of(core)
+    if rank is not None:
+        i = RK.index(k)
+        me = T.land[:, rank * W:(rank + 1) * W]
+        slot = T.hbuf[n_of[ch]]
+        g.sync.dma_start(T.xd[:], T.x[:]).then_inc(T.sem.ldx, 16)
+        g.sync.dma_start(me, T.x[:]).then_inc(T.sem.ldl, 16)
+        g.wait_ge(T.sem.ldx, 16)
+        peers = [ch * 8 + kk for kk in RK if kk != k]
+        g.remote_dma_fused([
+            RemoteDMATransfer(dst_ids=[did(mate * 8 + HK[i]), did(plane * 8 + HK[i])], dma_engine_mask=0x00FF,
+                              remote_sem=hsem(ch), srcs=[T.xd[:]], dsts=[slot, slot]),
+            RemoteDMATransfer(dst_ids=[did(p) for p in peers], dma_engine_mask=0xFF00,
+                              remote_sem=gsem(ch), srcs=[T.xd[:]], dsts=[me] * 3),
+        ], local_sem=T.sem.sent)
+        rid, pid, _se = topo.addr(diag * 8 + HK[i])
+        g.remote_dma(slot, T.xd[:], hsem(ch), T.sem.sent, pid, rid, 0x00FF)
+
+        plan = ((ch, g.sync, T.sem.st_a, 24), (mate, g.scalar, T.sem.st_b, 64),
+                (plane, g.sync, T.sem.st_a, 64), (diag, g.scalar, T.sem.st_b, 64))
+        g.sync.wait_ge(T.sem.ldl, 16)
+        for c, q, st, need in plan:
+            c0 = T.rank_of(c * 8 + RK[0]) * W
+            q.wait_ge(gsem(c), need)
+            q.dma_start(T.y[:, c0:c0 + 4 * W], T.land[:, c0:c0 + 4 * W]).then_inc(st, 16)
+        g.wait_ge(T.sem.sent, 24)
+        g.sync.wait_ge(T.sem.st_a, 32)
+        g.scalar.wait_ge(T.sem.st_b, 32)
+        return
+
+    j = HK.index(k)
+    ranks = [ch * 8 + RK[(j + s) % 4] for s in range(4)]
+    for c in (mate, plane, diag):
+        c0 = T.rank_of(c * 8 + RK[j]) * W
+        g.wait_ge(hsem(c), 8)
+        g.remote_dma_fused([
+            RemoteDMATransfer(dst_ids=[did(r) for r in ranks], dma_engine_mask=0xFFFF, remote_sem=gsem(c),
+                              srcs=[T.hbuf[n_of[c]]], dsts=[T.land[:, c0:c0 + W]] * 4),
+        ], local_sem=T.sem.sent)
+    g.wait_ge(T.sem.sent, 48)

@@ -25,6 +25,7 @@ def rank_program(g, core, T, topo):
     n_of = dict((c, n) for n, c in enumerate(chips))
     hsem = lambda c: T.sem["h%d" % n_of[c]]
     gsem = lambda c: T.sem["g%d" % n_of[c]]
+    cols = lambda c, i: T.land[:, T.rank_of(c * 8 + RK[i]) * W:(T.rank_of(c * 8 + RK[i]) + 1) * W]
 
     def did(c):
         rid, pid, _se = topo.addr(c)
@@ -33,40 +34,66 @@ def rank_program(g, core, T, topo):
     rank = T.rank_of(core)
     if rank is not None:
         i = RK.index(k)
-        me = T.land[:, rank * W:(rank + 1) * W]
+        b = i % 2 == 1
+        me = cols(ch, i)
         slot = T.hbuf[n_of[ch]]
+        peers = [did(ch * 8 + kk) for kk in RK if kk != k]
         g.sync.dma_start(T.xd[:], T.x[:]).then_inc(T.sem.ldx, 16)
         g.sync.dma_start(me, T.x[:]).then_inc(T.sem.ldl, 16)
         g.wait_ge(T.sem.ldx, 16)
-        peers = [ch * 8 + kk for kk in RK if kk != k]
+        if b:
+            far_ids, far_dsts = [did(plane * 8 + k), did(mate * 8 + HK[i])], [me, slot]
+        else:
+            far_ids, far_dsts = [did(mate * 8 + HK[i]), did(plane * 8 + HK[i])], [slot, slot]
         g.remote_dma_fused([
-            RemoteDMATransfer(dst_ids=[did(mate * 8 + HK[i]), did(plane * 8 + HK[i])], dma_engine_mask=0x00FF,
-                              remote_sem=hsem(ch), srcs=[T.xd[:]], dsts=[slot, slot]),
-            RemoteDMATransfer(dst_ids=[did(p) for p in peers], dma_engine_mask=0xFF00,
+            RemoteDMATransfer(dst_ids=far_ids, dma_engine_mask=0x00FF,
+                              remote_sem=hsem(ch), srcs=[T.xd[:]], dsts=far_dsts),
+            RemoteDMATransfer(dst_ids=peers, dma_engine_mask=0xFF00,
                               remote_sem=gsem(ch), srcs=[T.xd[:]], dsts=[me] * 3),
         ], local_sem=T.sem.sent)
-        rid, pid, _se = topo.addr(diag * 8 + HK[i])
-        g.remote_dma(slot, T.xd[:], hsem(ch), T.sem.sent, pid, rid, 0x00FF)
+        if b:
+            got = cols(plane, i)
+            g.wait_ge(hsem(plane), 8)
+            g.remote_dma_fused([
+                RemoteDMATransfer(dst_ids=[did(mate * 8 + HK[i])], dma_engine_mask=0x00FF,
+                                  remote_sem=hsem(plane), srcs=[got], dsts=[T.hbuf[n_of[plane]]]),
+                RemoteDMATransfer(dst_ids=peers, dma_engine_mask=0xFF00,
+                                  remote_sem=gsem(plane), srcs=[got], dsts=[got] * 3),
+            ], local_sem=T.sem.sent)
 
-        plan = ((ch, g.sync, T.sem.st_a, 24), (mate, g.scalar, T.sem.st_b, 64),
-                (plane, g.sync, T.sem.st_a, 64), (diag, g.scalar, T.sem.st_b, 64))
+        plan = ((ch, g.sync, T.sem.st_a, 24), (mate, g.scalar, T.sem.st_b, 48),
+                (plane, g.sync, T.sem.st_a, 40 if b else 48), (diag, g.scalar, T.sem.st_b, 64))
         g.sync.wait_ge(T.sem.ldl, 16)
         for c, q, st, need in plan:
             c0 = T.rank_of(c * 8 + RK[0]) * W
             q.wait_ge(gsem(c), need)
+            if b and c == plane:
+                q.wait_ge(hsem(plane), 8)
             q.dma_start(T.y[:, c0:c0 + 4 * W], T.land[:, c0:c0 + 4 * W]).then_inc(st, 16)
-        g.wait_ge(T.sem.sent, 24)
+        g.wait_ge(T.sem.sent, 32 if b else 16)
         g.sync.wait_ge(T.sem.st_a, 32)
         g.scalar.wait_ge(T.sem.st_b, 32)
         return
 
     j = HK.index(k)
-    ranks = [ch * 8 + RK[(j + s) % 4] for s in range(4)]
-    for c in (mate, plane, diag):
-        c0 = T.rank_of(c * 8 + RK[j]) * W
-        g.wait_ge(hsem(c), 8)
+    ranks = [did(ch * 8 + RK[(j + s) % 4]) for s in range(4)]
+    a = j % 2 == 0
+
+    def fan(c, mask):
+        return RemoteDMATransfer(dst_ids=ranks, dma_engine_mask=mask, remote_sem=gsem(c),
+                                 srcs=[T.hbuf[n_of[c]]], dsts=[cols(c, j)] * 4)
+
+    g.wait_ge(hsem(mate), 8)
+    if a:
         g.remote_dma_fused([
-            RemoteDMATransfer(dst_ids=[did(r) for r in ranks], dma_engine_mask=0xFFFF, remote_sem=gsem(c),
-                              srcs=[T.hbuf[n_of[c]]], dsts=[T.land[:, c0:c0 + W]] * 4),
+            RemoteDMATransfer(dst_ids=[did(plane * 8 + k)], dma_engine_mask=0x00FF, remote_sem=hsem(mate),
+                              srcs=[T.hbuf[n_of[mate]]], dsts=[T.hbuf[n_of[mate]]]),
+            fan(mate, 0xFF00),
         ], local_sem=T.sem.sent)
-    g.wait_ge(T.sem.sent, 48)
+        g.wait_ge(hsem(plane), 8)
+        g.remote_dma_fused([fan(plane, 0xFFFF)], local_sem=T.sem.sent)
+    else:
+        g.remote_dma_fused([fan(mate, 0xFFFF)], local_sem=T.sem.sent)
+    g.wait_ge(hsem(diag), 8)
+    g.remote_dma_fused([fan(diag, 0xFFFF)], local_sem=T.sem.sent)
+    g.wait_ge(T.sem.sent, 48 if a else 32)

@@ -3,6 +3,7 @@ from concourse.bass import DstId, RemoteDMATransfer
 W = 512
 RK = (2, 3, 6, 7)
 HK = (0, 1, 4, 5)
+B = (1, 3)
 
 SCRATCH = {
     "land": ("sbuf", [128, 16 * W], "bfloat16"),
@@ -34,7 +35,7 @@ def rank_program(g, core, T, topo):
     rank = T.rank_of(core)
     if rank is not None:
         i = RK.index(k)
-        b = i % 2 == 1
+        b = i in B
         me = cols(ch, i)
         slot = T.hbuf[n_of[ch]]
         peers = [did(ch * 8 + kk) for kk in RK if kk != k]
@@ -61,8 +62,10 @@ def rank_program(g, core, T, topo):
                                   remote_sem=gsem(plane), srcs=[got], dsts=[got] * 3),
             ], local_sem=T.sem.sent)
 
-        plan = ((ch, g.sync, T.sem.st_a, 24), (mate, g.scalar, T.sem.st_b, 48),
-                (plane, g.sync, T.sem.st_a, 40 if b else 48), (diag, g.scalar, T.sem.st_b, 64))
+        need_m = sum(16 if p in B else 8 for p in range(4))
+        need_p = sum((0 if p == i else 8) if p in B else 16 for p in range(4))
+        plan = ((ch, g.sync, T.sem.st_a, 24), (mate, g.scalar, T.sem.st_b, need_m),
+                (plane, g.sync, T.sem.st_a, need_p), (diag, g.scalar, T.sem.st_b, 64))
         g.sync.wait_ge(T.sem.ldl, 16)
         for c, q, st, need in plan:
             c0 = T.rank_of(c * 8 + RK[0]) * W
@@ -77,7 +80,7 @@ def rank_program(g, core, T, topo):
 
     j = HK.index(k)
     ranks = [did(ch * 8 + RK[(j + s) % 4]) for s in range(4)]
-    a = j % 2 == 0
+    a = j not in B
 
     def fan(c, mask):
         return RemoteDMATransfer(dst_ids=ranks, dma_engine_mask=mask, remote_sem=gsem(c),

from concourse.bass import DstId, RemoteDMATransfer

W = 512
RK = (2, 3, 6, 7)
HK = (0, 1, 4, 5)
B = (1, 3)

SCRATCH = {
    "land": ("sbuf", [128, 16 * W], "bfloat16"),
    "xd": ("dram", [128, W], "bfloat16"),
    "hbuf": ("dram", [4, 128, W], "bfloat16"),
}
SEMAPHORES = ["ldx", "ldl", "sent", "st_a", "st_b",
              "h0", "h1", "h2", "h3",
              "g0", "g1", "g2", "g3"]


def rank_program(g, core, T, topo):
    chips = sorted(set(topo.chip(c) for c in T.cores))
    ch, k = topo.chip(core), core % 8
    if ch not in chips:
        return
    mate = ch ^ 1
    plane = [c for c in chips if topo.same_plane(c, ch)][0]
    diag = plane ^ 1
    n_of = dict((c, n) for n, c in enumerate(chips))
    hsem = lambda c: T.sem["h%d" % n_of[c]]
    gsem = lambda c: T.sem["g%d" % n_of[c]]
    cols = lambda c, i: T.land[:, T.rank_of(c * 8 + RK[i]) * W:(T.rank_of(c * 8 + RK[i]) + 1) * W]

    def did(c):
        rid, pid, _se = topo.addr(c)
        return DstId(rid=rid, pnc=pid)

    rank = T.rank_of(core)
    if rank is not None:
        i = RK.index(k)
        b = i in B
        me = cols(ch, i)
        slot = T.hbuf[n_of[ch]]
        peers = [did(ch * 8 + kk) for kk in RK if kk != k]
        g.sync.dma_start(T.xd[:], T.x[:]).then_inc(T.sem.ldx, 16)
        g.sync.dma_start(me, T.x[:]).then_inc(T.sem.ldl, 16)
        g.wait_ge(T.sem.ldx, 16)
        if b:
            far_ids, far_dsts = [did(plane * 8 + k), did(mate * 8 + HK[i])], [me, slot]
        else:
            far_ids, far_dsts = [did(mate * 8 + HK[i]), did(plane * 8 + HK[i])], [slot, slot]
        g.remote_dma_fused([
            RemoteDMATransfer(dst_ids=far_ids, dma_engine_mask=0x00FF,
                              remote_sem=hsem(ch), srcs=[T.xd[:]], dsts=far_dsts),
            RemoteDMATransfer(dst_ids=peers, dma_engine_mask=0xFF00,
                              remote_sem=gsem(ch), srcs=[T.xd[:]], dsts=[me] * 3),
        ], local_sem=T.sem.sent)
        if b:
            got = cols(plane, i)
            g.wait_ge(hsem(plane), 8)
            g.remote_dma_fused([
                RemoteDMATransfer(dst_ids=[did(mate * 8 + HK[i])], dma_engine_mask=0x00FF,
                                  remote_sem=hsem(plane), srcs=[got], dsts=[T.hbuf[n_of[plane]]]),
                RemoteDMATransfer(dst_ids=peers, dma_engine_mask=0xFF00,
                                  remote_sem=gsem(plane), srcs=[got], dsts=[got] * 3),
            ], local_sem=T.sem.sent)

        need_m = sum(16 if p in B else 8 for p in range(4))
        need_p = sum((0 if p == i else 8) if p in B else 16 for p in range(4))
        plan = ((ch, g.sync, T.sem.st_a, 24), (mate, g.scalar, T.sem.st_b, need_m),
                (plane, g.sync, T.sem.st_a, need_p), (diag, g.scalar, T.sem.st_b, 64))
        g.sync.wait_ge(T.sem.ldl, 16)
        for c, q, st, need in plan:
            c0 = T.rank_of(c * 8 + RK[0]) * W
            q.wait_ge(gsem(c), need)
            if b and c == plane:
                q.wait_ge(hsem(plane), 8)
            q.dma_start(T.y[:, c0:c0 + 4 * W], T.land[:, c0:c0 + 4 * W]).then_inc(st, 16)
        g.wait_ge(T.sem.sent, 32 if b else 16)
        g.sync.wait_ge(T.sem.st_a, 32)
        g.scalar.wait_ge(T.sem.st_b, 32)
        return

    j = HK.index(k)
    ranks = [did(ch * 8 + RK[(j + s) % 4]) for s in range(4)]
    a = j not in B

    def fan(c, mask):
        return RemoteDMATransfer(dst_ids=ranks, dma_engine_mask=mask, remote_sem=gsem(c),
                                 srcs=[T.hbuf[n_of[c]]], dsts=[cols(c, j)] * 4)

    g.wait_ge(hsem(mate), 8)
    if a:
        g.remote_dma_fused([
            RemoteDMATransfer(dst_ids=[did(plane * 8 + k)], dma_engine_mask=0x00FF, remote_sem=hsem(mate),
                              srcs=[T.hbuf[n_of[mate]]], dsts=[T.hbuf[n_of[mate]]]),
            fan(mate, 0xFF00),
        ], local_sem=T.sem.sent)
        g.wait_ge(hsem(plane), 8)
        g.remote_dma_fused([fan(plane, 0xFFFF)], local_sem=T.sem.sent)
    else:
        g.remote_dma_fused([fan(mate, 0xFFFF)], local_sem=T.sem.sent)
    g.wait_ge(hsem(diag), 8)
    g.remote_dma_fused([fan(diag, 0xFFFF)], local_sem=T.sem.sent)
    g.wait_ge(T.sem.sent, 48 if a else 32)
